import numpy as np
CORES = [17,81,89,18,82,90]
N = 6
CAP = 256
T = N * CAP
def entries(a): return a.T.reshape(-1)
def pack(v, P): return np.ascontiguousarray(np.asarray(v, np.int32).reshape(-1, P).T)
def lists(rng, how):
    C = rng.integers(0, CAP + 1, (N, N))
    if how == "edge": C = np.array([0, 1, CAP - 1, CAP])[(rng.permutation(N)[:, None] + rng.permutation(N)[None, :]) % 4]
    if how == "full": C[:] = CAP
    if how == "lone": z = int(rng.integers(N)); k = C[z].copy(); C[:] = 0; C[z] = np.maximum(k, 1)
    if how == "none": u, v, w = rng.permutation(N)[:3]; C = np.maximum(C, 1); C[u] = 0; C[:, u] = 0; C[v] = 0; C[:, w] = 0
    if how == "zeros": C = rng.integers(4, CAP, (N, N))
    return {"cnt": np.stack([pack(np.concatenate([c, np.zeros(32 - N, np.int64)]), 16) for c in C])}
def setup_inputs(rng):
    return dict({"x": rng.standard_normal((N, 128, T), dtype=np.float32)}, **lists(rng, "uniform"))
def setup_inputs_edge(rng):
    d = setup_inputs(rng); d.update(lists(rng, "edge"))
    for k in ("x",): d[k] = (d[k].astype(np.float32) * 1048576.0).astype(d[k].dtype)
    return d
def setup_inputs_full(rng):
    d = setup_inputs(rng); d.update(lists(rng, "full"))
    for k in ("x",): d[k] = (d[k].astype(np.float32) * (1 / 1024.0)).astype(d[k].dtype)
    return d
def setup_inputs_lone(rng):
    d = setup_inputs(rng); d.update(lists(rng, "lone"))
    return d
def setup_inputs_none(rng):
    d = setup_inputs(rng); d.update(lists(rng, "none"))
    return d
def setup_inputs_zeros(rng):
    d = setup_inputs(rng); d.update(lists(rng, "zeros"))
    K = np.stack([entries(a) for a in d["cnt"]])[:, :N]; B = np.cumsum(K, axis=1) - K
    Z = np.concatenate([B, B + rng.integers(2, K - 1), B + K - 1], axis=1)
    for r in range(N): d["x"][r][:, Z[r]] = 0
    d["x"][:, 0][rng.random((N, T)) < 0.5] = 0
    return d
def check_inputs(x):
    bad = []
    if x["cnt"].min() < 0 or x["cnt"].max() >= CAP + 1: bad.append("cnt out of range")
    if any(entries(a)[N:].any() for a in x["cnt"]): bad.append("an entry from N on isn't 0")
    return bad
def reference(x, cnt):
    C = np.stack([entries(c)[:N] for c in cnt]); S = np.cumsum(C, axis=1) - C
    y = np.zeros((N, 128, T), x.dtype)
    for d in range(N):
        got = np.concatenate([x[r][:, S[r, d]:S[r, d] + C[r, d]] for r in range(N)], axis=1); y[d][:, :got.shape[1]] = got
    return {"y": y}

@@ -1,0 +1,299 @@
+from concourse.bass import DstId, RemoteDMATransfer
+from concourse.mybir import AluOpType as Op, ActivationFunctionType as Act
+
+N = 6
+CAP = 256
+COLS = N * CAP
+HALF = COLS // 2
+K = COLS // 16
+NSEM = 80
+
+SCRATCH = {
+    "xs": ("sbuf", [128, COLS], "float32"),
+    "sb": ("sbuf", [128, COLS], "float32"),
+    "land": ("sbuf", [128, COLS + 4], "float32"),
+    "yb": ("sbuf", [128, COLS], "float32"),
+    "cl": ("dram", [N, 128, 1], "int32"),
+    "ct": ("sbuf", [16, 2], "int32"),
+    "cs": ("sbuf", [N, 32], "int32"),
+    "ei": ("sbuf", [96, 128], "int32"),
+    "ea": ("sbuf", [96, 128], "int32"),
+    "em": ("sbuf", [96, 128], "bfloat16"),
+    "base": ("sbuf", [96, K], "float32"),
+    "ones": ("sbuf", [16, 128], "bfloat16"),
+    "c16": ("sbuf", [16, 1], "bfloat16"),
+    "qrow": ("sbuf", [1, 128], "bfloat16"),
+    "krow": ("sbuf", [1, K], "bfloat16"),
+    "krow2": ("sbuf", [1, K], "bfloat16"),
+    "pa": ("sbuf", [16, 1], "float32"),
+    "pb": ("sbuf", [16, 1], "float32"),
+    "pm": ("sbuf", [16, K], "bfloat16"),
+    "pm2": ("sbuf", [16, K], "bfloat16"),
+    "dm": ("sbuf", [16, K], "bfloat16"),
+    "cf": ("sbuf", [16, 1], "float32"),
+    "ru": ("sbuf", [16, K], "bfloat16"),
+    "cb": ("sbuf", [N, 1], "bfloat16"),
+    "stp": ("sbuf", [96, K], "bfloat16"),
+    "offs": ("sbuf", [128, K], "uint16"),
+    "offr": ("sbuf", [128, K], "uint16"),
+    "psS": ("psum", [128, 512], "float32"),
+    "psP": ("psum", [128, 512], "float32"),
+    "psW": ("psum", [128, 512], "float32"),
+    "psR": ("psum", [128, 512], "float32"),
+}
+SEMAPHORES = ["ca", "ls"] + ["d%d" % s for s in range(N)] + ["e%d" % i for i in range(NSEM)]
+
+CALLS = [
+    [[2, 5], [1, 4, 3]],
+    [[2, 5], [0, 3, 4]],
+    [[0, 1], [3, 4], [5]],
+    [[1, 2], [4, 5, 0]],
+    [[0, 2], [3, 5, 1]],
+    [[0, 1], [3, 4, 2]],
+]
+
+
+def bits(m):
+    return [e for e in range(16) if m >> e & 1]
+
+
+def tomask(es):
+    return sum(1 << e for e in es)
+
+
+def make_plan(cores, topo, ncores=96):
+    hop, help_ = {}, {}
+    for s in range(N):
+        for d in range(N):
+            a, b = cores[s], cores[d]
+            if a == b:
+                continue
+            if topo.may_write(a, b):
+                hop[s, d] = b
+                continue
+            ca, cb = topo.chip(a), topo.chip(b)
+            free = [h for h in range(ncores) if h not in cores and h not in help_
+                    and topo.may_write(a, h) and topo.may_write(h, b)]
+            mate_a = [c for c in range(ncores // 8) if topo.mates(c, ca)][0]
+            group_chips = [topo.chip(c) for c in cores]
+            far = [h for h in free if topo.mates(topo.chip(h), cb) and topo.same_plane(topo.chip(h), ca)
+                   and topo.chip(h) not in group_chips and topo.die(h) == topo.die(a)
+                   and not topo.may_write(h, a)  or (topo.mates(topo.chip(h), cb) and topo.same_plane(topo.chip(h), ca)
+                   and topo.chip(h) not in group_chips and topo.die(h) == topo.die(a))]
+            near = [h for h in free if topo.chip(h) == ca and topo.die(h) != topo.die(a)]
+            h = (far or near)[0]
+            hop[s, d] = h
+            help_[h] = (s, d)
+    return hop, help_
+
+
+def call_masks(core, hops, topo, offmask):
+    off = [i for i, h in enumerate(hops) if topo.chip(h) != topo.chip(core)]
+    on = [i for i, h in enumerate(hops) if topo.chip(h) == topo.chip(core)]
+    out = [0] * len(hops)
+    if off:
+        es = bits(offmask)
+        n = len(es) // len(off)
+        for q, i in enumerate(off):
+            out[i] = tomask(es[q * n:(q + 1) * n])
+    if on:
+        es = bits(topo.mask(core, hops[on[0]]))
+        if off:
+            es = [e for e in es if e not in bits(offmask)]
+        else:
+            es = es if len(on) > 1 else [e for e in es if e not in bits(offmask)]
+        n = len(es) // len(on)
+        for q, i in enumerate(on):
+            out[i] = tomask(es[q * n:(q + 1) * n])
+    return out
+
+
+def plan_all(cores, topo):
+    hop, help_ = make_plan(cores, topo)
+    calls = {}
+    arrive = {}
+    for r in range(N):
+        core = cores[r]
+        offmask = [topo.mask(core, hop[r, d]) for d in range(N) if d != r and topo.chip(hop[r, d]) != topo.chip(core)][0]
+        lst = []
+        for ds in CALLS[r]:
+            hops = [hop[r, d] for d in ds]
+            ms = call_masks(core, hops, topo, offmask)
+            lst.append(list(zip(ds, hops, ms)))
+            for h, m in zip(hops, ms):
+                arrive[h, r] = len(bits(m))
+        calls[r] = (lst, offmask)
+    for h, (s, d) in help_.items():
+        arrive[cores[d], s] = len(bits(topo.mask(h, cores[d])))
+    return hop, help_, calls, arrive
+
+
+def dst_id(c, topo):
+    rid, pid, _ = topo.addr(c)
+    return DstId(rid=rid, pnc=pid)
+
+
+def helper_program(g, core, T, topo, s, d, arrive):
+    dst = T.cores[d]
+    m = topo.mask(core, dst)
+    rid, pid, _ = topo.addr(dst)
+    g.wait_ge(T.sem.ca, 8)
+    g.remote_dma(T.cl[s], T.cl[s], T.sem.ca, T.sem.ls, pid, rid, m)
+    ds = T.sem["d%d" % s]
+    g.wait_ge(ds, arrive[core, s])
+    blk = T.land[:, s * CAP:(s + 1) * CAP]
+    g.remote_dma(blk, blk, ds, T.sem.ls, pid, rid, m)
+    g.wait_ge(T.sem.ls, 2 * len(bits(m)))
+
+
+def rank_program(g, core, T, topo):
+    cores = list(T.cores)
+    hop, help_, calls, arrive = plan_all(cores, topo)
+    r = T.rank_of(core)
+    if r is None:
+        if core in help_:
+            helper_program(g, core, T, topo, help_[core][0], help_[core][1], arrive)
+        return
+
+    Q = {"g": g, "v": g.vector, "s": g.scalar, "t": g.tensor, "y": g.sync}
+    used = [0]
+    waited = {}
+    seen = set()
+
+    def new():
+        used[0] += 1
+        return "e%d" % (used[0] - 1)
+
+    def wait(q, evs):
+        for nm, val in evs:
+            waited[nm] = True
+            if (q, nm, val) not in seen:
+                seen.add((q, nm, val))
+                Q[q].wait_ge(T.sem[nm], val)
+
+    pend = {}
+
+    def ev(inst, inc=1):
+        nm = new()
+        inst.then_inc(T.sem[nm], inc)
+        pend[nm] = inc
+        return (nm, inc)
+
+    ncl = new()
+    e_ct = ev(g.sync.dma_start(T.ct[:], T.cnt[:]), 16)
+    for a in range(4):
+        (g.sync if a == 0 else g.scalar).dma_start(T.cl[r, 32 * a:32 * a + 32, 0], T.cnt[:]).then_inc(T.sem[ncl], 16)
+    pend[ncl] = 64
+    e_cl = (ncl, 64)
+    e_x0 = ev(g.sync.dma_start(T.xs[:, 0:HALF], T.x[:, 0:HALF]), 16)
+    e_x1 = ev(g.scalar.dma_start(T.xs[:, HALF:COLS], T.x[:, HALF:COLS]), 16)
+
+    e_ei = ev(g.iota(T.ei[:], [[1, 128]], 0, 15))
+    e_base = ev(g.iota(T.base[:], [[16, K]], 0, 1, allow_small_or_imprecise_dtypes=True))
+    e_ones = ev(g.vector.memset(T.ones[:], 1.0))
+    e_c16 = ev(g.vector.memset(T.c16[:], 16.0))
+    e_zero = ev(g.vector.memset(T.land[:, COLS:COLS + 4], 0.0))
+    v = g.vector
+    wait("v", [e_ei])
+    e_ea = ev(v.tensor_scalar(T.ea[:], T.ei[:], 15, None, Op.bitwise_and))
+    wait("v", [e_base])
+    e_pb = ev(v.tensor_scalar(T.pb[:], T.base[0:16, 0:1], 31.0, 16.0, Op.mult, Op.add))
+    e_pa = ev(v.tensor_scalar(T.pa[:], T.base[0:16, 0:1], 31.0, None, Op.mult))
+    wait("v", [e_pb])
+    e_pm2 = ev(v.tensor_scalar(T.pm2[:], T.ei[0:16, 0:K], T.pb[:], None, Op.is_ge))
+    wait("v", [e_ea])
+    e_qrow = ev(v.tensor_copy(T.qrow[:], T.ea[0:1, :]))
+    e_krow2 = ev(v.tensor_scalar(T.krow2[:], T.ea[0:1, 0:K], 16.0, None, Op.mult))
+    e_em = ev(v.tensor_scalar(T.em[:], T.ea[:], 0.0, None, Op.is_equal))
+    e_krow = ev(v.tensor_copy(T.krow[:], T.base[0:1, :]))
+    wait("v", [e_pa])
+    e_pm = ev(v.tensor_scalar(T.pm[:], T.ei[0:16, 0:K], T.pa[:], None, Op.is_ge))
+    wait("v", [e_pm, e_pm2])
+    e_dm = ev(v.tensor_tensor(T.dm[:], T.pm2[:], T.pm[:], Op.subtract))
+
+    t = g.tensor
+    wait("t", [e_ones, e_qrow, e_krow2])
+    t.matmul(T.psS[:, 0:K], T.qrow[:], T.ones[0:1, 0:K], True, False)
+    t.matmul(T.psS[:, 0:K], T.ones[0:1, :], T.krow2[:], False, False)
+    wait("v", [e_ct])
+    e_cf = ev(v.tensor_copy(T.cf[:], T.ct[:, 0:1]))
+    wait("v", [e_cf])
+    e_ru = ev(v.tensor_scalar(T.ru[:], T.pm2[:], T.cf[:], None, Op.mult))
+    wait("t", [e_ru])
+    e_psS = ev(t.matmul(T.psS[:, 0:K], T.ones[:], T.ru[:], False, True))
+    wait("v", [e_psS])
+    e_offs = ev(v.tensor_copy(T.offs[:], T.psS[:, 0:K]))
+
+    lst, offmask = calls[r]
+    firsts = [hop[r, d] for d in range(N) if d != r]
+    on = [c for c in firsts if topo.chip(c) == topo.chip(core)]
+    off = [c for c in firsts if topo.chip(c) != topo.chip(core)]
+    nls = 0
+    trs = []
+    for grp, m in ((on, topo.mask(core, on[0]) & ~offmask), (off, offmask)):
+        trs.append(RemoteDMATransfer(dst_ids=[dst_id(c, topo) for c in grp], dma_engine_mask=m, remote_sem=T.sem.ca,
+                                     srcs=[T.cl[r]], dsts=[T.cl[r] for _ in grp]))
+        nls += len(bits(m))
+    wait("g", [e_cl])
+    g.remote_dma_fused(trs, local_sem=T.sem.ls)
+
+    order = [d for ds in CALLS[r] for d in ds] + [r]
+    e_pack = {}
+    for i, d in enumerate(order):
+        q = "v" if i % 2 == 0 else "s"
+        wait(q, [e_offs, e_x0] + ([e_x1] if (d + 1) * CAP > HALF else []))
+        out = T.land[:, d * CAP:(d + 1) * CAP] if d == r else T.sb[:, d * CAP:(d + 1) * CAP]
+        src = T.xs[:, 0:(d + 1) * CAP].indirect(T.offs[:, 16 * d:16 * d + 16])
+        e_pack[d] = ev(v.tensor_copy(out, src) if q == "v" else g.scalar.activation(out, src, Act.Copy))
+
+    for call in lst:
+        trs = []
+        for d, h, m in call:
+            wait("g", [e_pack[d]])
+            at = slice(r * CAP, (r + 1) * CAP)
+            trs.append(RemoteDMATransfer(dst_ids=[dst_id(h, topo)], dma_engine_mask=m, remote_sem=T.sem["d%d" % r],
+                                         srcs=[T.sb[:, d * CAP:(d + 1) * CAP]], dsts=[T.land[:, at]]))
+            nls += len(bits(m))
+        g.remote_dma_fused(trs, local_sem=T.sem.ls)
+
+    g.sync.wait_ge(T.sem.ca, 8 * (N - 1))
+    wait("y", [e_cl])
+    e_cs = ev(g.sync.dma_start(T.cs[:], T.cl[0:N, 0:32, 0]), 16)
+    wait("t", [e_c16, e_pm2, e_pm, e_dm, e_em, e_krow])
+    t.matmul(T.psP[0:96, 0:1], T.pm2[0:N, :], T.c16[0:N, :], True, False)
+    t.matmul(T.psW[0:96, 0:1], T.ones[0:16, 0:96], T.c16[:], True, False)
+    t.matmul(T.psR[:, 0:K], T.qrow[:], T.ones[0:1, 0:K], True, False)
+    t.matmul(T.psR[:, 0:K], T.ones[0:1, :], T.krow[:], False, False)
+    wait("v", [e_cs])
+    e_cb = ev(v.tensor_copy(T.cb[:], T.cs[:, 2 * r:2 * r + 1]))
+    wait("t", [e_cb])
+    e_psP = ev(t.matmul(T.psP[0:96, 0:1], T.pm[0:N, :], T.cb[:], False, True))
+    e_psW = ev(t.matmul(T.psW[0:96, 0:1], T.dm[0:N, :], T.cb[:], False, True))
+    wait("v", [e_psP, e_psW])
+    e_stp = ev(v.tensor_scalar(T.stp[:], T.base[:], T.psP[0:96, 0:1], T.psW[0:96, 0:1], Op.is_ge, Op.mult))
+    wait("t", [e_stp])
+    e_psR = ev(t.matmul(T.psR[:, 0:K], T.em[:], T.stp[:], False, True))
+    wait("v", [e_psR])
+    e_oA = ev(v.tensor_scalar(T.offr[:, K // 2:K], T.psR[:, K // 2:K], float(COLS), float(HALF), Op.min, Op.subtract))
+    e_oB = ev(v.tensor_scalar(T.offr[:, 0:K // 2], T.psR[:, 0:K // 2], float(COLS), None, Op.min))
+
+    for lo, e_o, srcs in ((HALF, e_oA, (3, 4, 5)), (0, e_oB, (0, 1, 2))):
+        need = [("d%d" % s, arrive[core, s]) for s in srcs if s != r] + [e_o, e_zero, e_pack[r]]
+        for i, q in enumerate(("v", "s")):
+            wait(q, need)
+            a = lo + i * HALF // 2
+            b = a + HALF // 2
+            src = T.land[:, lo:COLS + 4].indirect(T.offr[:, a // 16:b // 16])
+            if q == "v":
+                e = ev(v.tensor_copy(T.yb[:, a:b], src))
+                wait("y", [e])
+                ev(g.sync.dma_start(T.y[:, a:b], T.yb[:, a:b]), 16)
+            else:
+                e = ev(g.scalar.activation(T.yb[:, a:b], src, Act.Copy))
+                wait("s", [e])
+                ev(g.scalar.dma_start(T.y[:, a:b], T.yb[:, a:b]), 16)
+
+    g.wait_ge(T.sem.ls, nls)
+    for nm in list(pend):
+        if nm not in waited:
+            g.wait_ge(T.sem[nm], pend[nm])

@@ -44,13 +44,26 @@ SCRATCH = {
 SEMAPHORES = ["ca", "ls"] + ["d%d" % s for s in range(N)] + ["e%d" % i for i in range(NSEM)]
 
 CALLS = [
-    [[2, 5], [1, 4, 3]],
-    [[2, 5], [0, 3, 4]],
+    [[2, 1], [5, 4], [3]],
+    [[2, 0], [5, 3], [4]],
     [[0, 1], [3, 4], [5]],
     [[1, 2], [4, 5, 0]],
     [[0, 2], [3, 5, 1]],
     [[0, 1], [3, 4, 2]],
 ]
+PACK = [
+    ([2, 5, 3], [1, 4]),
+    ([2, 5, 4], [0, 3]),
+    ([0, 3, 5], [1, 4]),
+    ([1, 0, 4], [2, 5]),
+    ([0, 1, 3], [2, 5]),
+    ([0, 2, 3], [1, 4]),
+]
+VIA = {
+    (0, 2): "die", (0, 5): "die", (1, 2): "die", (1, 5): "die",
+    (2, 0): "mate", (2, 3): "mate", (2, 1): "die", (2, 4): "own",
+    (3, 1): "die", (4, 0): "die", (5, 0): "die",
+}
 
 
 def bits(m):
@@ -63,25 +76,24 @@ def tomask(es):
 
 def make_plan(cores, topo, ncores=96):
     hop, help_ = {}, {}
+    reach = {h: sum(1 for c in range(ncores) if c != h and topo.may_write(h, c)) for h in range(ncores)}
     for s in range(N):
         for d in range(N):
             a, b = cores[s], cores[d]
             if a == b:
                 continue
-            if topo.may_write(a, b):
-                hop[s, d] = b
+            hop[s, d] = b
+            if (s, d) not in VIA:
                 continue
+            how = VIA[s, d]
             ca, cb = topo.chip(a), topo.chip(b)
             free = [h for h in range(ncores) if h not in cores and h not in help_
                     and topo.may_write(a, h) and topo.may_write(h, b)]
-            mate_a = [c for c in range(ncores // 8) if topo.mates(c, ca)][0]
-            group_chips = [topo.chip(c) for c in cores]
-            far = [h for h in free if topo.mates(topo.chip(h), cb) and topo.same_plane(topo.chip(h), ca)
-                   and topo.chip(h) not in group_chips and topo.die(h) == topo.die(a)
-                   and not topo.may_write(h, a)  or (topo.mates(topo.chip(h), cb) and topo.same_plane(topo.chip(h), ca)
-                   and topo.chip(h) not in group_chips and topo.die(h) == topo.die(a))]
-            near = [h for h in free if topo.chip(h) == ca and topo.die(h) != topo.die(a)]
-            h = (far or near)[0]
+            if how == "mate":
+                free = [h for h in free if topo.mates(topo.chip(h), cb) and topo.die(h) == topo.die(a)]
+            else:
+                free = [h for h in free if topo.chip(h) == ca and (topo.die(h) == topo.die(a)) == (how == "own")]
+            h = sorted(free, key=lambda c: (reach[c], c))[0]
             hop[s, d] = h
             help_[h] = (s, d)
     return hop, help_
@@ -91,19 +103,10 @@ def call_masks(core, hops, topo, offmask):
     off = [i for i, h in enumerate(hops) if topo.chip(h) != topo.chip(core)]
     on = [i for i, h in enumerate(hops) if topo.chip(h) == topo.chip(core)]
     out = [0] * len(hops)
-    if off:
-        es = bits(offmask)
-        n = len(es) // len(off)
-        for q, i in enumerate(off):
-            out[i] = tomask(es[q * n:(q + 1) * n])
-    if on:
-        es = bits(topo.mask(core, hops[on[0]]))
-        if off:
-            es = [e for e in es if e not in bits(offmask)]
-        else:
-            es = es if len(on) > 1 else [e for e in es if e not in bits(offmask)]
-        n = len(es) // len(on)
-        for q, i in enumerate(on):
+    for grp, m in ((off, offmask), (on, topo.mask(core, hops[on[0]]) & ~offmask if on else 0)):
+        es = bits(m)
+        for q, i in enumerate(grp):
+            n = len(es) // len(grp)
             out[i] = tomask(es[q * n:(q + 1) * n])
     return out
 
@@ -159,6 +162,7 @@ def rank_program(g, core, T, topo):
     used = [0]
     waited = {}
     seen = set()
+    pend = {}
 
     def new():
         used[0] += 1
@@ -170,8 +174,6 @@ def rank_program(g, core, T, topo):
             if (q, nm, val) not in seen:
                 seen.add((q, nm, val))
                 Q[q].wait_ge(T.sem[nm], val)
-
-    pend = {}
 
     def ev(inst, inc=1):
         nm = new()
@@ -237,14 +239,13 @@ def rank_program(g, core, T, topo):
     wait("g", [e_cl])
     g.remote_dma_fused(trs, local_sem=T.sem.ls)
 
-    order = [d for ds in CALLS[r] for d in ds] + [r]
     e_pack = {}
-    for i, d in enumerate(order):
-        q = "v" if i % 2 == 0 else "s"
-        wait(q, [e_offs, e_x0] + ([e_x1] if (d + 1) * CAP > HALF else []))
-        out = T.land[:, d * CAP:(d + 1) * CAP] if d == r else T.sb[:, d * CAP:(d + 1) * CAP]
-        src = T.xs[:, 0:(d + 1) * CAP].indirect(T.offs[:, 16 * d:16 * d + 16])
-        e_pack[d] = ev(v.tensor_copy(out, src) if q == "v" else g.scalar.activation(out, src, Act.Copy))
+    for q, ds in (("v", PACK[r][0]), ("s", PACK[r][1] + [r])):
+        for d in ds:
+            wait(q, [e_offs, e_x0] + ([e_x1] if (d + 1) * CAP > HALF else []))
+            out = T.land[:, d * CAP:(d + 1) * CAP] if d == r else T.sb[:, d * CAP:(d + 1) * CAP]
+            src = T.xs[:, 0:(d + 1) * CAP].indirect(T.offs[:, 16 * d:16 * d + 16])
+            e_pack[d] = ev(v.tensor_copy(out, src) if q == "v" else g.scalar.activation(out, src, Act.Copy))
 
     for call in lst:
         trs = []

@@ -4,7 +4,6 @@ from concourse.mybir import AluOpType as Op, ActivationFunctionType as Act
 N = 6
 CAP = 256
 COLS = N * CAP
-HALF = COLS // 2
 K = COLS // 16
 NSEM = 80
 
@@ -16,6 +15,8 @@ SCRATCH = {
     "cl": ("dram", [N, 128, 1], "int32"),
     "ct": ("sbuf", [16, 2], "int32"),
     "cs": ("sbuf", [N, 32], "int32"),
+    "lc": ("sbuf", [128, 4], "int32"),
+    "lb": ("sbuf", [128, 1], "bfloat16"),
     "ei": ("sbuf", [96, 128], "int32"),
     "ea": ("sbuf", [96, 128], "int32"),
     "em": ("sbuf", [96, 128], "bfloat16"),
@@ -25,11 +26,19 @@ SCRATCH = {
     "qrow": ("sbuf", [1, 128], "bfloat16"),
     "krow": ("sbuf", [1, K], "bfloat16"),
     "krow2": ("sbuf", [1, K], "bfloat16"),
-    "pa": ("sbuf", [16, 1], "float32"),
     "pb": ("sbuf", [16, 1], "float32"),
+    "pp": ("sbuf", [96, 1], "float32"),
+    "pn": ("sbuf", [96, 1], "float32"),
+    "pq": ("sbuf", [96, 1], "int32"),
+    "pr": ("sbuf", [96, 1], "int32"),
+    "big": ("sbuf", [96, 1], "float32"),
+    "thr": ("sbuf", [96, 1], "float32"),
     "pm": ("sbuf", [16, K], "bfloat16"),
     "pm2": ("sbuf", [16, K], "bfloat16"),
     "dm": ("sbuf", [16, K], "bfloat16"),
+    "sp": ("sbuf", [96, K], "bfloat16"),
+    "sq": ("sbuf", [96, K], "bfloat16"),
+    "sw": ("sbuf", [96, K], "bfloat16"),
     "cf": ("sbuf", [16, 1], "float32"),
     "ru": ("sbuf", [16, K], "bfloat16"),
     "cb": ("sbuf", [N, 1], "bfloat16"),
@@ -41,23 +50,27 @@ SCRATCH = {
     "psW": ("psum", [128, 512], "float32"),
     "psR": ("psum", [128, 512], "float32"),
 }
-SEMAPHORES = ["ca", "ls"] + ["d%d" % s for s in range(N)] + ["e%d" % i for i in range(NSEM)]
+SEMAPHORES = ["ca", "cd", "ls"] + ["d%d" % s for s in range(N)] + ["e%d" % i for i in range(NSEM)]
 
+CUTS = [0, 768, COLS]
+NCE = 2
+STAGES = [(1024, 1536), (512, 1024), (0, 512)]
+STORE = "ysy"
 CALLS = [
     [[2, 1], [5, 4], [3]],
-    [[2, 0], [5, 3], [4]],
-    [[0, 1], [3, 4], [5]],
-    [[1, 2], [4, 5, 0]],
-    [[0, 2], [3, 5, 1]],
-    [[0, 1], [3, 4, 2]],
+    [[0], [2], [5, 3], [4]],
+    [[0], [1], [3, 4], [5]],
+    [[0], [1, 2], [5, 4]],
+    [[0], [2, 1], [3, 5]],
+    [[0], [1], [3, 4], [2]],
 ]
 PACK = [
-    ([2, 5, 3], [1, 4]),
-    ([2, 5, 4], [0, 3]),
-    ([0, 3, 5], [1, 4]),
-    ([1, 0, 4], [2, 5]),
-    ([0, 1, 3], [2, 5]),
-    ([0, 2, 3], [1, 4]),
+    ([2, 5, 3], [1, 4, 0]),
+    ([2, 5], [4, 3, 1]),
+    ([3, 5], [1, 4, 2]),
+    ([1, 4], [2, 5, 3]),
+    ([2, 3], [1, 5, 4]),
+    ([1, 4], [3, 2, 5]),
 ]
 VIA = {
     (0, 2): "die", (0, 5): "die", (1, 2): "die", (1, 5): "die",
@@ -115,6 +128,8 @@ def plan_all(cores, topo):
     hop, help_ = make_plan(cores, topo)
     calls = {}
     arrive = {}
+    cmask = {}
+    carrive = {}
     for r in range(N):
         core = cores[r]
         offmask = [topo.mask(core, hop[r, d]) for d in range(N) if d != r and topo.chip(hop[r, d]) != topo.chip(core)][0]
@@ -125,10 +140,17 @@ def plan_all(cores, topo):
             lst.append(list(zip(ds, hops, ms)))
             for h, m in zip(hops, ms):
                 arrive[h, r] = len(bits(m))
-        calls[r] = (lst, offmask)
+        calls[r] = lst
+        firsts = [hop[r, d] for d in range(N) if d != r]
+        on = [c for c in firsts if topo.chip(c) == topo.chip(core)]
+        off = [c for c in firsts if topo.chip(c) != topo.chip(core)]
+        cmask[r] = [(tomask(bits(topo.mask(core, on[0]) & ~offmask)[:NCE]), on), (tomask(bits(offmask)[:NCE]), off)]
+        for m, grp in cmask[r]:
+            for c in grp:
+                carrive[c] = carrive.get(c, 0) + len(bits(m))
     for h, (s, d) in help_.items():
         arrive[cores[d], s] = len(bits(topo.mask(h, cores[d])))
-    return hop, help_, calls, arrive
+    return hop, help_, calls, arrive, cmask, carrive
 
 
 def dst_id(c, topo):
@@ -136,12 +158,18 @@ def dst_id(c, topo):
     return DstId(rid=rid, pnc=pid)
 
 
-def helper_program(g, core, T, topo, s, d, arrive):
+def late_of(d, cores, hop):
+    return [s for s in range(N) if s != d and hop[s, d] != cores[d]]
+
+
+def helper_program(g, core, T, topo, s, d, plan):
+    hop, help_, calls, arrive, cmask, carrive = plan
     dst = T.cores[d]
     m = topo.mask(core, dst)
     rid, pid, _ = topo.addr(dst)
-    g.wait_ge(T.sem.ca, 8)
-    g.remote_dma(T.cl[s], T.cl[s], T.sem.ca, T.sem.ls, pid, rid, m)
+    q = late_of(d, list(T.cores), hop).index(s)
+    g.wait_ge(T.sem.ca, carrive[core])
+    g.remote_dma(T.lc[:, q:q + 1], T.cl[s], T.sem.cd, T.sem.ls, pid, rid, m)
     ds = T.sem["d%d" % s]
     g.wait_ge(ds, arrive[core, s])
     blk = T.land[:, s * CAP:(s + 1) * CAP]
@@ -151,11 +179,12 @@ def helper_program(g, core, T, topo, s, d, arrive):
 
 def rank_program(g, core, T, topo):
     cores = list(T.cores)
-    hop, help_, calls, arrive = plan_all(cores, topo)
+    plan = plan_all(cores, topo)
+    hop, help_, calls, arrive, cmask, carrive = plan
     r = T.rank_of(core)
     if r is None:
         if core in help_:
-            helper_program(g, core, T, topo, help_[core][0], help_[core][1], arrive)
+            helper_program(g, core, T, topo, help_[core][0], help_[core][1], plan)
         return
 
     Q = {"g": g, "v": g.vector, "s": g.scalar, "t": g.tensor, "y": g.sync}
@@ -181,58 +210,60 @@ def rank_program(g, core, T, topo):
         pend[nm] = inc
         return (nm, inc)
 
+    v, t = g.vector, g.tensor
+    late = late_of(r, cores, hop)
+    nl = len(late)
+    early = [s for s in range(N) if s not in late]
+
     ncl = new()
-    e_ct = ev(g.sync.dma_start(T.ct[:], T.cnt[:]), 16)
     for a in range(4):
-        (g.sync if a == 0 else g.scalar).dma_start(T.cl[r, 32 * a:32 * a + 32, 0], T.cnt[:]).then_inc(T.sem[ncl], 16)
+        (g.sync if a % 2 == 0 else g.scalar).dma_start(T.cl[r, 32 * a:32 * a + 32, 0], T.cnt[:]).then_inc(T.sem[ncl], 16)
     pend[ncl] = 64
     e_cl = (ncl, 64)
-    e_x0 = ev(g.sync.dma_start(T.xs[:, 0:HALF], T.x[:, 0:HALF]), 16)
-    e_x1 = ev(g.scalar.dma_start(T.xs[:, HALF:COLS], T.x[:, HALF:COLS]), 16)
+    e_ct = ev(g.sync.dma_start(T.ct[:], T.cnt[:]), 16)
+    e_x = []
+    for a, b in zip(CUTS, CUTS[1:]):
+        e_x.append((b, ev(g.scalar.dma_start(T.xs[:, a:b], T.x[:, a:b]), 16)))
+
+    def upto(n):
+        out = []
+        for b, e in e_x:
+            out.append(e)
+            if b >= n:
+                break
+        return out
 
     e_ei = ev(g.iota(T.ei[:], [[1, 128]], 0, 15))
-    e_base = ev(g.iota(T.base[:], [[16, K]], 0, 1, allow_small_or_imprecise_dtypes=True))
-    e_ones = ev(g.vector.memset(T.ones[:], 1.0))
-    e_c16 = ev(g.vector.memset(T.c16[:], 16.0))
-    e_zero = ev(g.vector.memset(T.land[:, COLS:COLS + 4], 0.0))
-    v = g.vector
+    e_pb = ev(g.iota(T.pb[:], [[0, 1]], 16, 31, allow_small_or_imprecise_dtypes=True))
+    e_pp = ev(g.iota(T.pp[:], [[0, 1]], 0, 1, allow_small_or_imprecise_dtypes=True))
+    e_pq = ev(g.iota(T.pq[:], [[0, 1]], 32 - 2 * r, 1))
+    e_ones = ev(v.memset(T.ones[:], 1.0))
+    e_c16 = ev(v.memset(T.c16[:], 16.0))
+    e_zero = ev(v.memset(T.land[:, COLS:COLS + 4], 0.0))
+    e_cs0 = ev(v.memset(T.cs[:], 0))
     wait("v", [e_ei])
     e_ea = ev(v.tensor_scalar(T.ea[:], T.ei[:], 15, None, Op.bitwise_and))
-    wait("v", [e_base])
-    e_pb = ev(v.tensor_scalar(T.pb[:], T.base[0:16, 0:1], 31.0, 16.0, Op.mult, Op.add))
-    e_pa = ev(v.tensor_scalar(T.pa[:], T.base[0:16, 0:1], 31.0, None, Op.mult))
     wait("v", [e_pb])
     e_pm2 = ev(v.tensor_scalar(T.pm2[:], T.ei[0:16, 0:K], T.pb[:], None, Op.is_ge))
     wait("v", [e_ea])
     e_qrow = ev(v.tensor_copy(T.qrow[:], T.ea[0:1, :]))
     e_krow2 = ev(v.tensor_scalar(T.krow2[:], T.ea[0:1, 0:K], 16.0, None, Op.mult))
-    e_em = ev(v.tensor_scalar(T.em[:], T.ea[:], 0.0, None, Op.is_equal))
-    e_krow = ev(v.tensor_copy(T.krow[:], T.base[0:1, :]))
-    wait("v", [e_pa])
-    e_pm = ev(v.tensor_scalar(T.pm[:], T.ei[0:16, 0:K], T.pa[:], None, Op.is_ge))
-    wait("v", [e_pm, e_pm2])
-    e_dm = ev(v.tensor_tensor(T.dm[:], T.pm2[:], T.pm[:], Op.subtract))
 
-    t = g.tensor
+    wait("v", [e_ct])
+    e_cf = ev(v.tensor_copy(T.cf[:], T.ct[:, 0:1]))
+    wait("v", [e_cf, e_pm2])
+    e_ru = ev(v.tensor_scalar(T.ru[:], T.pm2[:], T.cf[:], None, Op.mult))
     wait("t", [e_ones, e_qrow, e_krow2])
     t.matmul(T.psS[:, 0:K], T.qrow[:], T.ones[0:1, 0:K], True, False)
     t.matmul(T.psS[:, 0:K], T.ones[0:1, :], T.krow2[:], False, False)
-    wait("v", [e_ct])
-    e_cf = ev(v.tensor_copy(T.cf[:], T.ct[:, 0:1]))
-    wait("v", [e_cf])
-    e_ru = ev(v.tensor_scalar(T.ru[:], T.pm2[:], T.cf[:], None, Op.mult))
     wait("t", [e_ru])
     e_psS = ev(t.matmul(T.psS[:, 0:K], T.ones[:], T.ru[:], False, True))
     wait("v", [e_psS])
     e_offs = ev(v.tensor_copy(T.offs[:], T.psS[:, 0:K]))
 
-    lst, offmask = calls[r]
-    firsts = [hop[r, d] for d in range(N) if d != r]
-    on = [c for c in firsts if topo.chip(c) == topo.chip(core)]
-    off = [c for c in firsts if topo.chip(c) != topo.chip(core)]
     nls = 0
     trs = []
-    for grp, m in ((on, topo.mask(core, on[0]) & ~offmask), (off, offmask)):
+    for m, grp in cmask[r]:
         trs.append(RemoteDMATransfer(dst_ids=[dst_id(c, topo) for c in grp], dma_engine_mask=m, remote_sem=T.sem.ca,
                                      srcs=[T.cl[r]], dsts=[T.cl[r] for _ in grp]))
         nls += len(bits(m))
@@ -240,59 +271,109 @@ def rank_program(g, core, T, topo):
     g.remote_dma_fused(trs, local_sem=T.sem.ls)
 
     e_pack = {}
-    for q, ds in (("v", PACK[r][0]), ("s", PACK[r][1] + [r])):
+    for q, ds in (("v", PACK[r][0]), ("s", PACK[r][1])):
         for d in ds:
-            wait(q, [e_offs, e_x0] + ([e_x1] if (d + 1) * CAP > HALF else []))
             out = T.land[:, d * CAP:(d + 1) * CAP] if d == r else T.sb[:, d * CAP:(d + 1) * CAP]
-            src = T.xs[:, 0:(d + 1) * CAP].indirect(T.offs[:, 16 * d:16 * d + 16])
+            if d == 0:
+                wait(q, upto(CAP))
+                src = T.xs[:, 0:CAP]
+            else:
+                wait(q, [e_offs] + upto((d + 1) * CAP))
+                src = T.xs[:, 0:(d + 1) * CAP].indirect(T.offs[:, 16 * d:16 * d + 16])
             e_pack[d] = ev(v.tensor_copy(out, src) if q == "v" else g.scalar.activation(out, src, Act.Copy))
 
-    for call in lst:
+    for call in calls[r]:
         trs = []
         for d, h, m in call:
-            wait("g", [e_pack[d]])
+            wait("g", upto(CAP) if d == 0 else [e_pack[d]])
             at = slice(r * CAP, (r + 1) * CAP)
+            src = T.xs[:, 0:CAP] if d == 0 else T.sb[:, d * CAP:(d + 1) * CAP]
             trs.append(RemoteDMATransfer(dst_ids=[dst_id(h, topo)], dma_engine_mask=m, remote_sem=T.sem["d%d" % r],
-                                         srcs=[T.sb[:, d * CAP:(d + 1) * CAP]], dsts=[T.land[:, at]]))
+                                         srcs=[src], dsts=[T.land[:, at]]))
             nls += len(bits(m))
         g.remote_dma_fused(trs, local_sem=T.sem.ls)
 
-    g.sync.wait_ge(T.sem.ca, 8 * (N - 1))
-    wait("y", [e_cl])
-    e_cs = ev(g.sync.dma_start(T.cs[:], T.cl[0:N, 0:32, 0]), 16)
+    e_krow = ev(v.tensor_scalar(T.krow[:], T.ei[0:1, 0:K], 16.0, None, Op.mult))
+    e_em = ev(v.tensor_scalar(T.em[:], T.ea[:], 0.0, None, Op.is_equal))
+    e_pm = ev(v.tensor_scalar(T.pm[:], T.ei[0:16, 0:K], T.pb[:], -16.0, Op.subtract, Op.is_ge))
+    wait("v", [e_pp, e_pq])
+    e_pr = ev(v.tensor_scalar(T.pr[:], T.pq[:], 31, None, Op.bitwise_and))
+    e_pn = ev(v.tensor_scalar(T.pn[:], T.pp[:], -239.0, None, Op.mult))
+    wait("v", [e_pm])
+    e_dm = ev(v.tensor_tensor(T.dm[:], T.pm2[:], T.pm[:], Op.subtract))
+    wait("v", [e_pn])
+    e_base = ev(v.tensor_scalar(T.base[:], T.ei[:, 0:K], 16.0, T.pn[:], Op.mult, Op.add))
+    wait("v", [e_pr])
+    e_big = ev(v.tensor_scalar(T.big[:], T.pr[:], 0.0, 100000.0, Op.not_equal, Op.mult))
+    wait("v", [e_big])
+    e_thr = ev(v.tensor_scalar(T.thr[:], T.pp[:], 15.0, T.big[:], Op.mult, Op.add))
+    wait("v", [e_thr])
+    e_sp = []
+    for i, s in enumerate(late):
+        rows = slice(32 * i, 32 * i + 32)
+        for buf, lim in ((T.sp, 16.0 * s), (T.sq, 16.0 * s + 16.0)):
+            e_sp.append(ev(v.tensor_scalar(buf[rows, :], T.ei[rows, 0:K], T.thr[rows, :], lim, Op.subtract, Op.is_ge)))
+    wait("v", e_sp)
+    KL = 32 * nl
+    e_sw = ev(v.tensor_tensor(T.sw[0:KL, :], T.sq[0:KL, :], T.sp[0:KL, :], Op.subtract))
+
+    g.sync.wait_ge(T.sem.ca, carrive[core])
+    wait("y", [e_cl, e_cs0])
+    ncs = new()
+    k = 0
+    for s in early:
+        if s - 1 in early:
+            continue
+        e = s + 1
+        while e in early:
+            e += 1
+        g.sync.dma_start(T.cs[s:e, :], T.cl[s:e, 0:32, 0]).then_inc(T.sem[ncs], 16)
+        k += 16
+    pend[ncs] = k
     wait("t", [e_c16, e_pm2, e_pm, e_dm, e_em, e_krow])
-    t.matmul(T.psP[0:96, 0:1], T.pm2[0:N, :], T.c16[0:N, :], True, False)
-    t.matmul(T.psW[0:96, 0:1], T.ones[0:16, 0:96], T.c16[:], True, False)
     t.matmul(T.psR[:, 0:K], T.qrow[:], T.ones[0:1, 0:K], True, False)
     t.matmul(T.psR[:, 0:K], T.ones[0:1, :], T.krow[:], False, False)
-    wait("v", [e_cs])
+    t.matmul(T.psP[0:96, 0:1], T.pm2[0:N, :], T.c16[0:N, :], True, False)
+    t.matmul(T.psW[0:96, 0:1], T.ones[0:16, 0:96], T.c16[:], True, False)
+    wait("v", [(ncs, k)])
     e_cb = ev(v.tensor_copy(T.cb[:], T.cs[:, 2 * r:2 * r + 1]))
     wait("t", [e_cb])
-    e_psP = ev(t.matmul(T.psP[0:96, 0:1], T.pm[0:N, :], T.cb[:], False, True))
-    e_psW = ev(t.matmul(T.psW[0:96, 0:1], T.dm[0:N, :], T.cb[:], False, True))
-    wait("v", [e_psP, e_psW])
+    t.matmul(T.psP[0:96, 0:1], T.pm[0:N, :], T.cb[:], False, False)
+    t.matmul(T.psW[0:96, 0:1], T.dm[0:N, :], T.cb[:], False, False)
+    v.wait_ge(T.sem.cd, sum(len(bits(topo.mask(hop[s, r], core))) for s in late))
+    e_lb = []
+    for i in range(nl):
+        rows = slice(32 * i, 32 * i + 32)
+        e_lb.append(ev(v.tensor_copy(T.lb[rows, :], T.lc[rows, i:i + 1])))
+    wait("t", e_sp + [e_sw] + e_lb)
+    e_psP = ev(t.matmul(T.psP[0:96, 0:1], T.sp[0:KL, :], T.lb[0:KL, :], False, True))
+    e_psW = ev(t.matmul(T.psW[0:96, 0:1], T.sw[0:KL, :], T.lb[0:KL, :], False, True))
+    wait("v", [e_base, e_psP, e_psW])
     e_stp = ev(v.tensor_scalar(T.stp[:], T.base[:], T.psP[0:96, 0:1], T.psW[0:96, 0:1], Op.is_ge, Op.mult))
     wait("t", [e_stp])
     e_psR = ev(t.matmul(T.psR[:, 0:K], T.em[:], T.stp[:], False, True))
     wait("v", [e_psR])
-    e_oA = ev(v.tensor_scalar(T.offr[:, K // 2:K], T.psR[:, K // 2:K], float(COLS), float(HALF), Op.min, Op.subtract))
-    e_oB = ev(v.tensor_scalar(T.offr[:, 0:K // 2], T.psR[:, 0:K // 2], float(COLS), None, Op.min))
+    e_o = []
+    for lo, hi in STAGES:
+        a, b = lo // 16, hi // 16
+        if lo:
+            e_o.append(ev(v.tensor_scalar(T.offr[:, a:b], T.psR[:, a:b], float(COLS), float(lo), Op.min, Op.subtract)))
+        else:
+            e_o.append(ev(v.tensor_scalar(T.offr[:, a:b], T.psR[:, a:b], float(COLS), None, Op.min)))
 
-    for lo, e_o, srcs in ((HALF, e_oA, (3, 4, 5)), (0, e_oB, (0, 1, 2))):
-        need = [("d%d" % s, arrive[core, s]) for s in srcs if s != r] + [e_o, e_zero, e_pack[r]]
-        for i, q in enumerate(("v", "s")):
+    got = set()
+    for i, (lo, hi) in enumerate(STAGES):
+        srcs = [s for s in range(lo // CAP, N) if s not in got]
+        got |= set(srcs)
+        need = [("d%d" % s, arrive[core, s]) for s in srcs if s != r] + [e_o[i], e_zero] + ([e_pack[r]] if r in srcs else [])
+        mid = (lo + hi) // 2
+        es = []
+        for q, a, b in (("v", lo, mid), ("s", mid, hi)):
             wait(q, need)
-            a = lo + i * HALF // 2
-            b = a + HALF // 2
             src = T.land[:, lo:COLS + 4].indirect(T.offr[:, a // 16:b // 16])
-            if q == "v":
-                e = ev(v.tensor_copy(T.yb[:, a:b], src))
-                wait("y", [e])
-                ev(g.sync.dma_start(T.y[:, a:b], T.yb[:, a:b]), 16)
-            else:
-                e = ev(g.scalar.activation(T.yb[:, a:b], src, Act.Copy))
-                wait("s", [e])
-                ev(g.scalar.dma_start(T.y[:, a:b], T.yb[:, a:b]), 16)
+            es.append(ev(v.tensor_copy(T.yb[:, a:b], src) if q == "v" else g.scalar.activation(T.yb[:, a:b], src, Act.Copy)))
+        wait(STORE[i], es)
+        ev(Q[STORE[i]].dma_start(T.y[:, lo:hi], T.yb[:, lo:hi]), 16)
 
     g.wait_ge(T.sem.ls, nls)
     for nm in list(pend):

from concourse.bass import DstId, RemoteDMATransfer
from concourse.mybir import AluOpType as Op, ActivationFunctionType as Act

N = 6
CAP = 256
COLS = N * CAP
K = COLS // 16
NSEM = 80

SCRATCH = {
    "xs": ("sbuf", [128, COLS], "float32"),
    "sb": ("sbuf", [128, COLS], "float32"),
    "land": ("sbuf", [128, COLS + 4], "float32"),
    "yb": ("sbuf", [128, COLS], "float32"),
    "cl": ("dram", [N, 128, 1], "int32"),
    "ct": ("sbuf", [16, 2], "int32"),
    "cs": ("sbuf", [N, 32], "int32"),
    "lc": ("sbuf", [128, 4], "int32"),
    "lb": ("sbuf", [128, 1], "bfloat16"),
    "ei": ("sbuf", [96, 128], "int32"),
    "ea": ("sbuf", [96, 128], "int32"),
    "em": ("sbuf", [96, 128], "bfloat16"),
    "base": ("sbuf", [96, K], "float32"),
    "ones": ("sbuf", [16, 128], "bfloat16"),
    "c16": ("sbuf", [16, 1], "bfloat16"),
    "qrow": ("sbuf", [1, 128], "bfloat16"),
    "krow": ("sbuf", [1, K], "bfloat16"),
    "krow2": ("sbuf", [1, K], "bfloat16"),
    "pb": ("sbuf", [16, 1], "float32"),
    "pp": ("sbuf", [96, 1], "float32"),
    "pn": ("sbuf", [96, 1], "float32"),
    "pq": ("sbuf", [96, 1], "int32"),
    "pr": ("sbuf", [96, 1], "int32"),
    "big": ("sbuf", [96, 1], "float32"),
    "thr": ("sbuf", [96, 1], "float32"),
    "pm": ("sbuf", [16, K], "bfloat16"),
    "pm2": ("sbuf", [16, K], "bfloat16"),
    "dm": ("sbuf", [16, K], "bfloat16"),
    "sp": ("sbuf", [96, K], "bfloat16"),
    "sq": ("sbuf", [96, K], "bfloat16"),
    "sw": ("sbuf", [96, K], "bfloat16"),
    "cf": ("sbuf", [16, 1], "float32"),
    "ru": ("sbuf", [16, K], "bfloat16"),
    "cb": ("sbuf", [N, 1], "bfloat16"),
    "stp": ("sbuf", [96, K], "bfloat16"),
    "offs": ("sbuf", [128, K], "uint16"),
    "offr": ("sbuf", [128, K], "uint16"),
    "psS": ("psum", [128, 512], "float32"),
    "psP": ("psum", [128, 512], "float32"),
    "psW": ("psum", [128, 512], "float32"),
    "psR": ("psum", [128, 512], "float32"),
}
SEMAPHORES = ["ca", "cd", "ls"] + ["d%d" % s for s in range(N)] + ["e%d" % i for i in range(NSEM)]

CUTS = [0, 768, COLS]
NCE = 2
STAGES = [(1024, 1536), (512, 1024), (0, 512)]
STORE = "ysy"
CALLS = [
    [[2, 1], [5, 4], [3]],
    [[0], [2], [5, 3], [4]],
    [[0], [1], [3, 4], [5]],
    [[0], [1, 2], [5, 4]],
    [[0], [2, 1], [3, 5]],
    [[0], [1], [3, 4], [2]],
]
PACK = [
    ([2, 5, 3], [1, 4, 0]),
    ([2, 5], [4, 3, 1]),
    ([3, 5], [1, 4, 2]),
    ([1, 4], [2, 5, 3]),
    ([2, 3], [1, 5, 4]),
    ([1, 4], [3, 2, 5]),
]
VIA = {
    (0, 2): "die", (0, 5): "die", (1, 2): "die", (1, 5): "die",
    (2, 0): "mate", (2, 3): "mate", (2, 1): "die", (2, 4): "own",
    (3, 1): "die", (4, 0): "die", (5, 0): "die",
}


def bits(m):
    return [e for e in range(16) if m >> e & 1]


def tomask(es):
    return sum(1 << e for e in es)


def make_plan(cores, topo, ncores=96):
    hop, help_ = {}, {}
    reach = {h: sum(1 for c in range(ncores) if c != h and topo.may_write(h, c)) for h in range(ncores)}
    for s in range(N):
        for d in range(N):
            a, b = cores[s], cores[d]
            if a == b:
                continue
            hop[s, d] = b
            if (s, d) not in VIA:
                continue
            how = VIA[s, d]
            ca, cb = topo.chip(a), topo.chip(b)
            free = [h for h in range(ncores) if h not in cores and h not in help_
                    and topo.may_write(a, h) and topo.may_write(h, b)]
            if how == "mate":
                free = [h for h in free if topo.mates(topo.chip(h), cb) and topo.die(h) == topo.die(a)]
            else:
                free = [h for h in free if topo.chip(h) == ca and (topo.die(h) == topo.die(a)) == (how == "own")]
            h = sorted(free, key=lambda c: (reach[c], c))[0]
            hop[s, d] = h
            help_[h] = (s, d)
    return hop, help_


def call_masks(core, hops, topo, offmask):
    off = [i for i, h in enumerate(hops) if topo.chip(h) != topo.chip(core)]
    on = [i for i, h in enumerate(hops) if topo.chip(h) == topo.chip(core)]
    out = [0] * len(hops)
    for grp, m in ((off, offmask), (on, topo.mask(core, hops[on[0]]) & ~offmask if on else 0)):
        es = bits(m)
        for q, i in enumerate(grp):
            n = len(es) // len(grp)
            out[i] = tomask(es[q * n:(q + 1) * n])
    return out


def plan_all(cores, topo):
    hop, help_ = make_plan(cores, topo)
    calls = {}
    arrive = {}
    cmask = {}
    carrive = {}
    for r in range(N):
        core = cores[r]
        offmask = [topo.mask(core, hop[r, d]) for d in range(N) if d != r and topo.chip(hop[r, d]) != topo.chip(core)][0]
        lst = []
        for ds in CALLS[r]:
            hops = [hop[r, d] for d in ds]
            ms = call_masks(core, hops, topo, offmask)
            lst.append(list(zip(ds, hops, ms)))
            for h, m in zip(hops, ms):
                arrive[h, r] = len(bits(m))
        calls[r] = lst
        firsts = [hop[r, d] for d in range(N) if d != r]
        on = [c for c in firsts if topo.chip(c) == topo.chip(core)]
        off = [c for c in firsts if topo.chip(c) != topo.chip(core)]
        cmask[r] = [(tomask(bits(topo.mask(core, on[0]) & ~offmask)[:NCE]), on), (tomask(bits(offmask)[:NCE]), off)]
        for m, grp in cmask[r]:
            for c in grp:
                carrive[c] = carrive.get(c, 0) + len(bits(m))
    for h, (s, d) in help_.items():
        arrive[cores[d], s] = len(bits(topo.mask(h, cores[d])))
    return hop, help_, calls, arrive, cmask, carrive


def dst_id(c, topo):
    rid, pid, _ = topo.addr(c)
    return DstId(rid=rid, pnc=pid)


def late_of(d, cores, hop):
    return [s for s in range(N) if s != d and hop[s, d] != cores[d]]


def helper_program(g, core, T, topo, s, d, plan):
    hop, help_, calls, arrive, cmask, carrive = plan
    dst = T.cores[d]
    m = topo.mask(core, dst)
    rid, pid, _ = topo.addr(dst)
    q = late_of(d, list(T.cores), hop).index(s)
    g.wait_ge(T.sem.ca, carrive[core])
    g.remote_dma(T.lc[:, q:q + 1], T.cl[s], T.sem.cd, T.sem.ls, pid, rid, m)
    ds = T.sem["d%d" % s]
    g.wait_ge(ds, arrive[core, s])
    blk = T.land[:, s * CAP:(s + 1) * CAP]
    g.remote_dma(blk, blk, ds, T.sem.ls, pid, rid, m)
    g.wait_ge(T.sem.ls, 2 * len(bits(m)))


def rank_program(g, core, T, topo):
    cores = list(T.cores)
    plan = plan_all(cores, topo)
    hop, help_, calls, arrive, cmask, carrive = plan
    r = T.rank_of(core)
    if r is None:
        if core in help_:
            helper_program(g, core, T, topo, help_[core][0], help_[core][1], plan)
        return

    Q = {"g": g, "v": g.vector, "s": g.scalar, "t": g.tensor, "y": g.sync}
    used = [0]
    waited = {}
    seen = set()
    pend = {}

    def new():
        used[0] += 1
        return "e%d" % (used[0] - 1)

    def wait(q, evs):
        for nm, val in evs:
            waited[nm] = True
            if (q, nm, val) not in seen:
                seen.add((q, nm, val))
                Q[q].wait_ge(T.sem[nm], val)

    def ev(inst, inc=1):
        nm = new()
        inst.then_inc(T.sem[nm], inc)
        pend[nm] = inc
        return (nm, inc)

    v, t = g.vector, g.tensor
    late = late_of(r, cores, hop)
    nl = len(late)
    early = [s for s in range(N) if s not in late]

    ncl = new()
    for a in range(4):
        (g.sync if a % 2 == 0 else g.scalar).dma_start(T.cl[r, 32 * a:32 * a + 32, 0], T.cnt[:]).then_inc(T.sem[ncl], 16)
    pend[ncl] = 64
    e_cl = (ncl, 64)
    e_ct = ev(g.sync.dma_start(T.ct[:], T.cnt[:]), 16)
    e_x = []
    for a, b in zip(CUTS, CUTS[1:]):
        e_x.append((b, ev(g.scalar.dma_start(T.xs[:, a:b], T.x[:, a:b]), 16)))

    def upto(n):
        out = []
        for b, e in e_x:
            out.append(e)
            if b >= n:
                break
        return out

    e_ei = ev(g.iota(T.ei[:], [[1, 128]], 0, 15))
    e_pb = ev(g.iota(T.pb[:], [[0, 1]], 16, 31, allow_small_or_imprecise_dtypes=True))
    e_pp = ev(g.iota(T.pp[:], [[0, 1]], 0, 1, allow_small_or_imprecise_dtypes=True))
    e_pq = ev(g.iota(T.pq[:], [[0, 1]], 32 - 2 * r, 1))
    e_ones = ev(v.memset(T.ones[:], 1.0))
    e_c16 = ev(v.memset(T.c16[:], 16.0))
    e_zero = ev(v.memset(T.land[:, COLS:COLS + 4], 0.0))
    e_cs0 = ev(v.memset(T.cs[:], 0))
    wait("v", [e_ei])
    e_ea = ev(v.tensor_scalar(T.ea[:], T.ei[:], 15, None, Op.bitwise_and))
    wait("v", [e_pb])
    e_pm2 = ev(v.tensor_scalar(T.pm2[:], T.ei[0:16, 0:K], T.pb[:], None, Op.is_ge))
    wait("v", [e_ea])
    e_qrow = ev(v.tensor_copy(T.qrow[:], T.ea[0:1, :]))
    e_krow2 = ev(v.tensor_scalar(T.krow2[:], T.ea[0:1, 0:K], 16.0, None, Op.mult))

    wait("v", [e_ct])
    e_cf = ev(v.tensor_copy(T.cf[:], T.ct[:, 0:1]))
    wait("v", [e_cf, e_pm2])
    e_ru = ev(v.tensor_scalar(T.ru[:], T.pm2[:], T.cf[:], None, Op.mult))
    wait("t", [e_ones, e_qrow, e_krow2])
    t.matmul(T.psS[:, 0:K], T.qrow[:], T.ones[0:1, 0:K], True, False)
    t.matmul(T.psS[:, 0:K], T.ones[0:1, :], T.krow2[:], False, False)
    wait("t", [e_ru])
    e_psS = ev(t.matmul(T.psS[:, 0:K], T.ones[:], T.ru[:], False, True))
    wait("v", [e_psS])
    e_offs = ev(v.tensor_copy(T.offs[:], T.psS[:, 0:K]))

    nls = 0
    trs = []
    for m, grp in cmask[r]:
        trs.append(RemoteDMATransfer(dst_ids=[dst_id(c, topo) for c in grp], dma_engine_mask=m, remote_sem=T.sem.ca,
                                     srcs=[T.cl[r]], dsts=[T.cl[r] for _ in grp]))
        nls += len(bits(m))
    wait("g", [e_cl])
    g.remote_dma_fused(trs, local_sem=T.sem.ls)

    e_pack = {}
    for q, ds in (("v", PACK[r][0]), ("s", PACK[r][1])):
        for d in ds:
            out = T.land[:, d * CAP:(d + 1) * CAP] if d == r else T.sb[:, d * CAP:(d + 1) * CAP]
            if d == 0:
                wait(q, upto(CAP))
                src = T.xs[:, 0:CAP]
            else:
                wait(q, [e_offs] + upto((d + 1) * CAP))
                src = T.xs[:, 0:(d + 1) * CAP].indirect(T.offs[:, 16 * d:16 * d + 16])
            e_pack[d] = ev(v.tensor_copy(out, src) if q == "v" else g.scalar.activation(out, src, Act.Copy))

    for call in calls[r]:
        trs = []
        for d, h, m in call:
            wait("g", upto(CAP) if d == 0 else [e_pack[d]])
            at = slice(r * CAP, (r + 1) * CAP)
            src = T.xs[:, 0:CAP] if d == 0 else T.sb[:, d * CAP:(d + 1) * CAP]
            trs.append(RemoteDMATransfer(dst_ids=[dst_id(h, topo)], dma_engine_mask=m, remote_sem=T.sem["d%d" % r],
                                         srcs=[src], dsts=[T.land[:, at]]))
            nls += len(bits(m))
        g.remote_dma_fused(trs, local_sem=T.sem.ls)

    e_krow = ev(v.tensor_scalar(T.krow[:], T.ei[0:1, 0:K], 16.0, None, Op.mult))
    e_em = ev(v.tensor_scalar(T.em[:], T.ea[:], 0.0, None, Op.is_equal))
    e_pm = ev(v.tensor_scalar(T.pm[:], T.ei[0:16, 0:K], T.pb[:], -16.0, Op.subtract, Op.is_ge))
    wait("v", [e_pp, e_pq])
    e_pr = ev(v.tensor_scalar(T.pr[:], T.pq[:], 31, None, Op.bitwise_and))
    e_pn = ev(v.tensor_scalar(T.pn[:], T.pp[:], -239.0, None, Op.mult))
    wait("v", [e_pm])
    e_dm = ev(v.tensor_tensor(T.dm[:], T.pm2[:], T.pm[:], Op.subtract))
    wait("v", [e_pn])
    e_base = ev(v.tensor_scalar(T.base[:], T.ei[:, 0:K], 16.0, T.pn[:], Op.mult, Op.add))
    wait("v", [e_pr])
    e_big = ev(v.tensor_scalar(T.big[:], T.pr[:], 0.0, 100000.0, Op.not_equal, Op.mult))
    wait("v", [e_big])
    e_thr = ev(v.tensor_scalar(T.thr[:], T.pp[:], 15.0, T.big[:], Op.mult, Op.add))
    wait("v", [e_thr])
    e_sp = []
    for i, s in enumerate(late):
        rows = slice(32 * i, 32 * i + 32)
        for buf, lim in ((T.sp, 16.0 * s), (T.sq, 16.0 * s + 16.0)):
            e_sp.append(ev(v.tensor_scalar(buf[rows, :], T.ei[rows, 0:K], T.thr[rows, :], lim, Op.subtract, Op.is_ge)))
    wait("v", e_sp)
    KL = 32 * nl
    e_sw = ev(v.tensor_tensor(T.sw[0:KL, :], T.sq[0:KL, :], T.sp[0:KL, :], Op.subtract))

    g.sync.wait_ge(T.sem.ca, carrive[core])
    wait("y", [e_cl, e_cs0])
    ncs = new()
    k = 0
    for s in early:
        if s - 1 in early:
            continue
        e = s + 1
        while e in early:
            e += 1
        g.sync.dma_start(T.cs[s:e, :], T.cl[s:e, 0:32, 0]).then_inc(T.sem[ncs], 16)
        k += 16
    pend[ncs] = k
    wait("t", [e_c16, e_pm2, e_pm, e_dm, e_em, e_krow])
    t.matmul(T.psR[:, 0:K], T.qrow[:], T.ones[0:1, 0:K], True, False)
    t.matmul(T.psR[:, 0:K], T.ones[0:1, :], T.krow[:], False, False)
    t.matmul(T.psP[0:96, 0:1], T.pm2[0:N, :], T.c16[0:N, :], True, False)
    t.matmul(T.psW[0:96, 0:1], T.ones[0:16, 0:96], T.c16[:], True, False)
    wait("v", [(ncs, k)])
    e_cb = ev(v.tensor_copy(T.cb[:], T.cs[:, 2 * r:2 * r + 1]))
    wait("t", [e_cb])
    t.matmul(T.psP[0:96, 0:1], T.pm[0:N, :], T.cb[:], False, False)
    t.matmul(T.psW[0:96, 0:1], T.dm[0:N, :], T.cb[:], False, False)
    v.wait_ge(T.sem.cd, sum(len(bits(topo.mask(hop[s, r], core))) for s in late))
    e_lb = []
    for i in range(nl):
        rows = slice(32 * i, 32 * i + 32)
        e_lb.append(ev(v.tensor_copy(T.lb[rows, :], T.lc[rows, i:i + 1])))
    wait("t", e_sp + [e_sw] + e_lb)
    e_psP = ev(t.matmul(T.psP[0:96, 0:1], T.sp[0:KL, :], T.lb[0:KL, :], False, True))
    e_psW = ev(t.matmul(T.psW[0:96, 0:1], T.sw[0:KL, :], T.lb[0:KL, :], False, True))
    wait("v", [e_base, e_psP, e_psW])
    e_stp = ev(v.tensor_scalar(T.stp[:], T.base[:], T.psP[0:96, 0:1], T.psW[0:96, 0:1], Op.is_ge, Op.mult))
    wait("t", [e_stp])
    e_psR = ev(t.matmul(T.psR[:, 0:K], T.em[:], T.stp[:], False, True))
    wait("v", [e_psR])
    e_o = []
    for lo, hi in STAGES:
        a, b = lo // 16, hi // 16
        if lo:
            e_o.append(ev(v.tensor_scalar(T.offr[:, a:b], T.psR[:, a:b], float(COLS), float(lo), Op.min, Op.subtract)))
        else:
            e_o.append(ev(v.tensor_scalar(T.offr[:, a:b], T.psR[:, a:b], float(COLS), None, Op.min)))

    got = set()
    for i, (lo, hi) in enumerate(STAGES):
        srcs = [s for s in range(lo // CAP, N) if s not in got]
        got |= set(srcs)
        need = [("d%d" % s, arrive[core, s]) for s in srcs if s != r] + [e_o[i], e_zero] + ([e_pack[r]] if r in srcs else [])
        mid = (lo + hi) // 2
        es = []
        for q, a, b in (("v", lo, mid), ("s", mid, hi)):
            wait(q, need)
            src = T.land[:, lo:COLS + 4].indirect(T.offr[:, a // 16:b // 16])
            es.append(ev(v.tensor_copy(T.yb[:, a:b], src) if q == "v" else g.scalar.activation(T.yb[:, a:b], src, Act.Copy)))
        wait(STORE[i], es)
        ev(Q[STORE[i]].dma_start(T.y[:, lo:hi], T.yb[:, lo:hi]), 16)

    g.wait_ge(T.sem.ls, nls)
    for nm in list(pend):
        if nm not in waited:
            g.wait_ge(T.sem[nm], pend[nm])
